import numpy as np
import ml_dtypes


def mxq(x, axis, fmt="e4m3"):
    dtype, down = {"e4m3": (ml_dtypes.float8_e4m3fn, 7), "e5m2": (ml_dtypes.float8_e5m2, 14)}[fmt]
    v = np.moveaxis(np.asarray(x, np.float32).astype(ml_dtypes.bfloat16).astype(np.float64), axis, -1)
    blocks = v.reshape(v.shape[:-1] + (-1, 32))
    amax = np.abs(blocks).max(-1, keepdims=True)
    byte = np.maximum(np.where(amax > 0, np.frexp(amax)[1] - 1 + 127, 0) - down, 1)
    scale = np.exp2(byte - 127.0)
    codes = (blocks / scale).astype(np.float32).astype(dtype).astype(np.float64)
    return np.moveaxis((codes * scale).reshape(v.shape), -1, axis)


WIDE = False


def mx_kscale(k):
    if not WIDE:
        return np.ones(k)
    levels = np.array([10, -10, 5, -5, 0])
    if k % 512:
        return np.exp2(np.random.permutation(np.resize(levels, k // 32))).repeat(32)
    a = np.empty((k // 512, 16))
    for p in range(k // 512):
        a[p, :8] = np.random.permutation(np.resize(levels, 8))
        for g in range(8):
            far = levels[np.abs(levels - a[p, g]) >= 10]
            a[p, g + 8] = far[np.random.randint(len(far))]
    return np.exp2(a.ravel()).repeat(32)


def f64(x):
    return np.asarray(x).astype(np.float64)


def striped(idx):
    return np.tile(idx.reshape(-1, 16).T, (8, 1)).astype(np.uint16)


def unstriped(offs):
    return offs[:16].T.reshape(-1).astype(np.int64)


E2M1 = np.array([0.0, 0.5, 1.0, 1.5, 2.0, 3.0, 4.0, 6.0, -0.0, -0.5, -1.0, -1.5, -2.0, -3.0, -4.0, -6.0])


def pack_weight(w, fmt):
    k, n = w.shape
    w = f64(np.asarray(w, np.float32).astype(ml_dtypes.bfloat16)).reshape(k // 32, 32, n)
    amax = np.abs(w).max(1)
    if fmt == "e4m3":
        byte = np.frexp(amax)[1] - 1 + 127 - 7
    else:
        mant, ex = np.frexp(amax / 6.0)
        byte = np.where(mant > 0.5, ex, ex - 1) + 127
    byte = np.clip(np.where(amax > 0, byte, 1), 1, 254)
    scaled = (w * np.exp2(127.0 - byte)[:, None, :]).reshape(k, n).astype(np.float32)
    by_word = np.ascontiguousarray(scaled.reshape(k // 512, 128, 4, n).transpose(0, 1, 3, 2))
    if fmt == "e4m3":
        words = by_word.astype(ml_dtypes.float8_e4m3fn).view(np.uint8)
    else:
        c = by_word.astype(ml_dtypes.float4_e2m1fn).view(np.uint8) & 0xF
        words = (c[..., 0::2] | (c[..., 1::2] << 4)).reshape(k // 512, 128, 2 * n)
    return np.ascontiguousarray(words), np.ascontiguousarray(byte.astype(np.uint8).reshape(k // 512, 16, n))


def unpack_weight(words, scales, fmt):
    g, _, n = scales.shape
    words = np.ascontiguousarray(words).reshape(g, 128, n, -1)
    if fmt == "e4m3":
        vals = words.view(ml_dtypes.float8_e4m3fn).astype(np.float64)
    else:
        nib = np.empty((g, 128, n, 4), np.uint8)
        nib[..., 0::2] = words & 0xF
        nib[..., 1::2] = words >> 4
        vals = E2M1[nib]
    vals = vals * np.repeat(np.exp2(scales.astype(np.float64) - 127.0), 8, axis=1)[..., None]
    return vals.transpose(0, 1, 3, 2).reshape(g * 512, n)


def relu(v):
    return np.maximum(v, 0.0)


K, T, E, C, H, N, HOT = 1536, 512, 6, 256, 512, 512, 3
TOP = 3


def by_expert(wq, xq):
    return np.concatenate([wq[e].T @ xq[:, e * C:(e + 1) * C] for e in range(E)], axis=1)


def setup_inputs():
    n = np.random.standard_normal
    s = mx_kscale(K)
    u = mx_kscale(H)
    deal = np.repeat(np.arange(E), C).reshape(TOP, T)[:, np.random.permutation(T)]
    deal = np.take_along_axis(deal, np.argsort(np.random.rand(TOP, T), axis=0), axis=0)
    for _ in range(8):
        s_, t_ = np.random.permutation(T).reshape(2, -1); r = np.random.randint(TOP, size=T // 2); x, y = deal[r, s_].copy(), deal[r, t_].copy()
        ok = ~((deal[:, s_] == y).any(0) | (deal[:, t_] == x).any(0)); deal[r[ok], s_[ok]] = y[ok]; deal[r[ok], t_[ok]] = x[ok]
    order = np.lexsort((np.random.rand(TOP * T), deal.reshape(-1)))
    slot_token = order % T; pos = np.empty(TOP * T, np.int64); pos[order] = np.arange(TOP * T); pos = pos.reshape(TOP, T)
    g = np.random.uniform(0.5, 1.5, (TOP, T)); g = g / g.sum(0)
    x = pack_weight(n((K, T)) * s[:, None], "e4m3")
    w1h = [pack_weight(m, "e4m3") for m in n((HOT, K, H)) / np.sqrt(K) / s[None, :, None] * u]
    w2h = [pack_weight(m, "e4m3") for m in n((HOT, H, N)) / np.sqrt(H) / u[None, :, None]]
    w1c = [pack_weight(m, "e2m1") for m in n((E - HOT, K, H)) / np.sqrt(K) / s[None, :, None] * u]
    w2c = [pack_weight(m, "e2m1") for m in n((E - HOT, H, N)) / np.sqrt(H) / u[None, :, None]]
    return {
        "x_words": x[0],
        "x_scales": x[1],
        "w1h_words": np.stack([m[0] for m in w1h]),
        "w1h_scales": np.stack([m[1] for m in w1h]),
        "w2h_words": np.stack([m[0] for m in w2h]),
        "w2h_scales": np.stack([m[1] for m in w2h]),
        "w1c_words": np.stack([m[0] for m in w1c]),
        "w1c_scales": np.stack([m[1] for m in w1c]),
        "w2c_words": np.stack([m[0] for m in w2c]),
        "w2c_scales": np.stack([m[1] for m in w2c]),
        "gate": np.stack([np.tile(r, (128, 1)) for r in g]).astype(np.float32),
        "offs": striped(slot_token),
        "pos1": striped(pos[0]),
        "pos2": striped(pos[1]),
        "pos3": striped(pos[2]),
    }


def reference(x_words, x_scales, w1h_words, w1h_scales, w2h_words, w2h_scales, w1c_words, w1c_scales, w2c_words, w2c_scales, gate, offs, pos1, pos2, pos3):
    w1h = np.stack([unpack_weight(w1h_words[e], w1h_scales[e], "e4m3") for e in range(HOT)])
    w2h = np.stack([unpack_weight(w2h_words[e], w2h_scales[e], "e4m3") for e in range(HOT)])
    w1c = np.stack([unpack_weight(w1c_words[e], w1c_scales[e], "e2m1") for e in range(E - HOT)])
    w2c = np.stack([unpack_weight(w2c_words[e], w2c_scales[e], "e2m1") for e in range(E - HOT)])
    idx = unstriped(offs)
    xq = unpack_weight(x_words, x_scales, "e4m3")[:, idx]
    w1 = [*w1h, *w1c]
    w2 = [*w2h, *w2c]
    h = relu(by_expert(w1, xq))
    y = by_expert(w2, mxq(h, 0, "e4m3"))
    out = sum(f64(gate[r, :1]) * y[:, unstriped(p)] for r, p in enumerate((pos1, pos2, pos3)))
    return out

@@ -1,0 +1,294 @@
+from contextlib import ExitStack
+
+import concourse.mybir as mybir
+from concourse.masks import make_identity
+
+K, T, E, C, H, N, HOT, TOP = 1536, 512, 6, 256, 512, 512, 3, 3
+COLD = E - HOT
+S = E * C
+P = 128
+PASSES = K // 512
+FLOPS = 2 * S * (K * H + H * N)
+
+F32 = mybir.dt.float32
+BF16 = mybir.dt.bfloat16
+I32 = mybir.dt.int32
+U32 = mybir.dt.uint32
+U16 = mybir.dt.uint16
+U8 = mybir.dt.uint8
+FP8X4 = mybir.dt.float8_e4m3fn_x4
+FP4X4 = mybir.dt.float4_e2m1fn_x4
+RELU = mybir.ActivationFunctionType.Relu
+MULT = mybir.AluOpType.mult
+ADD = mybir.AluOpType.add
+
+W1H_ROW = 4
+W2H_ROW = 8
+SHIFT_ROWS = 112
+
+
+def tile_moe_hot_mlp_relu_kernel(
+    tc, x_words, x_scales, w1h_words, w1h_scales, w2h_words, w2h_scales,
+    w1c_words, w1c_scales, w2c_words, w2c_scales, gate, offs, pos1, pos2, pos3, out,
+):
+    nc = tc.nc
+    with ExitStack() as ctx:
+        lists = ctx.enter_context(tc.tile_pool(name="lists", bufs=1))
+        keep = ctx.enter_context(tc.tile_pool(name="keep", bufs=1))
+        big = ctx.enter_context(tc.tile_pool(name="big", bufs=4))
+        ring = ctx.enter_context(tc.tile_pool(name="ring", bufs=4))
+        acc = ctx.enter_context(tc.psum_pool(name="acc", bufs=5))
+        turn = ctx.enter_context(tc.psum_pool(name="turn", bufs=3))
+
+        def held(shape, dtype, name):
+            return keep.tile(shape, dtype, name=name, align_bytes=64)
+
+        def zeroed_plane(width, name):
+            plane = held([P, width], U8, name)
+            nc.vector.memset(plane[:].bitcast(I32), 0)
+            return plane
+
+        def load_scale_rows(plane, row, scales):
+            rows = scales.bitcast(I32).rearrange("e s b i -> b (e s) i")
+            view = plane.bitcast(I32).rearrange("p (a i) -> p a i", i=H // 4)
+            for q in range(4):
+                nc.sync.dma_start(out=view[32 * q + row : 32 * q + row + 4], in_=rows[4 * q : 4 * q + 4])
+
+        x_plane = zeroed_plane(T, "x_plane")
+        w1h_plane = zeroed_plane(HOT * PASSES * H, "w1h_plane")
+        w1c_plane = zeroed_plane(COLD * PASSES * H, "w1c_plane")
+        cold_planes = [zeroed_plane(COLD * C, f"cold_plane{s}") for s in range(1, PASSES)]
+        ident = held([P, P], F32, "ident")
+        make_identity(nc, ident[:])
+
+        offsets = lists.tile([P, S // 16], U16, name="offsets")
+        nc.sync.dma_start(offsets[:], offs)
+        x_win = [held([P, T], I32, f"x_win{s}") for s in range(PASSES)]
+
+        def load_tokens(s):
+            nc.sync.dma_start(out=x_win[s][:], in_=x_words[s].rearrange("p t d -> p (t d)").bitcast(I32))
+
+        def w1_tile(e):
+            return big.tile([P, PASSES, H if e < HOT else H // 2], I32, name=f"w1_{e}", tag="big", align_bytes=64)
+
+        def w1_source(e):
+            if e < HOT:
+                return w1h_words[e].rearrange("s p i d -> p s (i d)").bitcast(I32)
+            return w1c_words[e - HOT].rearrange("s p b -> p s b").bitcast(I32)
+
+        for s in range(PASSES):
+            load_tokens(s)
+        w1 = [w1_tile(0)]
+        nc.sync.dma_start(out=w1[0][:, 0:1, :], in_=w1_source(0)[:, 0:1, :])
+        for q in range(4):
+            nc.sync.dma_start(
+                out=x_plane[:].bitcast(I32)[32 * q : 32 * q + 4 * PASSES, :],
+                in_=x_scales.bitcast(I32)[:, 4 * q : 4 * q + 4, :],
+            )
+        load_scale_rows(w1h_plane[:], W1H_ROW, w1h_scales)
+        nc.sync.dma_start(out=w1[0][:, 1:PASSES, :], in_=w1_source(0)[:, 1:PASSES, :])
+
+        def load_w1(e):
+            w1.append(w1_tile(e))
+            nc.sync.dma_start(out=w1[e][:], in_=w1_source(e))
+
+        load_w1(1)
+        load_scale_rows(w1c_plane[:], 0, w1c_scales)
+        load_w1(2)
+        load_w1(3)
+
+        def slots_of(first, count):
+            return offsets[:, first // 16 : (first + count) // 16]
+
+        tok_words = {}
+        tok_bytes = {}
+
+        def gather_words(e, s):
+            words = ring.tile([P, C], U32, name="tok", align_bytes=64)
+            tok_words[e, s] = words
+            step = P if (e, s) == (E - 1, PASSES - 1) else C
+            for first in range(0, C, step):
+                nc.vector.tensor_copy(
+                    words[:, first : first + step],
+                    x_win[s][:].bitcast(U32).indirect(slots_of(e * C + first, step)),
+                )
+
+        def gather_bytes(e, tile, col):
+            tok_bytes[e] = (tile, col)
+            nc.vector.tensor_copy(tile[:, col : col + C], x_plane[:].indirect(slots_of(e * C, C)))
+
+        def byte_tile():
+            return ring.tile([P, 2 * C], U8, name="tok_bytes", bufs=2, align_bytes=64)
+
+        def shift_rows(first, count):
+            tile, col = tok_bytes[first]
+            dst = (first - HOT) * C
+            for s in range(1, PASSES):
+                nc.sync.dma_start(
+                    out=cold_planes[s - 1][:, dst : dst + count * C].bitcast(I32)[0:SHIFT_ROWS, :],
+                    in_=tile[:, col : col + count * C].bitcast(I32)[4 * s : 4 * s + SHIFT_ROWS, :],
+                )
+
+        def gathers(e):
+            if e in (0, 1, 2, 4):
+                tile = byte_tile()
+                gather_bytes(e, tile, 0)
+            gather_words(e, 0)
+            if e in (2, 4):
+                gather_bytes(e + 1, tile, C)
+                if e == 2:
+                    shift_rows(3, 1)
+                else:
+                    shift_rows(4, 2)
+            for s in range(1, PASSES):
+                gather_words(e, s)
+
+        pos = []
+        for r, src in enumerate((pos1, pos2, pos3)):
+            lst = lists.tile([P, T // 16], U16, name=f"pos{r}")
+            nc.sync.dma_start(lst[:], src)
+            pos.append(lst)
+
+        def first_layer(e):
+            banks = [acc.tile([P, H], F32, name="acc") for j in range(2)]
+            for s in range(PASSES):
+                for j in range(2):
+                    cols = slice(j * P, (j + 1) * P)
+                    w_cols = slice((e % HOT * PASSES + s) * H, (e % HOT * PASSES + s + 1) * H)
+                    if e < HOT:
+                        tok_scale = tok_bytes[e][0][4 * s : P, cols]
+                        w_op = w1[e][:, s, :].bitcast(FP8X4)
+                        w_scale = w1h_plane[W1H_ROW:P, w_cols]
+                    else:
+                        if s == 0:
+                            plane, first = tok_bytes[e]
+                        else:
+                            plane, first = cold_planes[s - 1], (e - HOT) * C
+                        tok_scale = plane[:, first + j * P : first + (j + 1) * P]
+                        w_op = w1[e][:, s, :].bitcast(FP4X4)
+                        w_scale = w1c_plane[:, w_cols]
+                    nc.tensor.matmul_mx(
+                        out=banks[j][:], lhsT=tok_words[e, s][:, cols].bitcast(FP8X4), lhsT_scale=tok_scale,
+                        rhs=w_op, rhs_scale=w_scale, start=(s == 0), stop=(s == PASSES - 1),
+                    )
+            hidden = []
+            for j in range(2):
+                hb = held([P, H], BF16, f"hb{e}_{j}")
+                nc.scalar.activation(
+                    out=hb[:].rearrange("t (u p d) -> t u p d", u=2, d=2),
+                    in_=banks[j][:].rearrange("t (p u d) -> t u p d", u=2, d=2),
+                    func=RELU,
+                )
+                hidden.append(hb)
+            return hidden
+
+        def turn_hidden(tiles, name):
+            n = len(tiles)
+            bank = turn.tile([P, 4 * P], F32, name="turn")
+            for j, hb in enumerate(tiles):
+                words = hb[:].bitcast(F32)
+                for u in range(2):
+                    col = (2 * j + u) * P
+                    nc.tensor.transpose(bank[:, col : col + P], words[:, u * P : (u + 1) * P], ident[:])
+            grouped = held([P, n * H], BF16, name)
+            nc.scalar.copy(
+                out=grouped[:].bitcast(F32).rearrange("p (j t u) -> p j t u", j=n, u=2),
+                in_=bank[:, 0 : 2 * n * P].rearrange("p (j u t) -> p j t u", j=n, u=2),
+            )
+            return grouped
+
+        pieces = []
+        pending = None
+        for e in range(E):
+            gathers(e)
+            hidden = first_layer(e)
+            if e + 4 < E:
+                load_w1(e + 4)
+            if e == 0:
+                w2_plane = w1h_plane[:, 0 : HOT * N]
+                load_scale_rows(w2_plane, W2H_ROW, w2h_scales)
+                load_scale_rows(w2_plane, 0, w2c_scales)
+            if pending is not None:
+                pieces.append((e - 1, 0, C, turn_hidden(pending, f"grouped{e - 1}")))
+            pending = hidden
+        for j in range(2):
+            pieces.append((E - 1, j * P, P, turn_hidden(pending[j : j + 1], f"grouped_last{j}")))
+
+        w2h = big.tile([P, HOT, N], I32, name="w2h", tag="big", align_bytes=64)
+        nc.sync.dma_start(out=w2h[:], in_=w2h_words.rearrange("e s p n d -> p (e s) (n d)").bitcast(I32))
+        w2c = big.tile([P, COLD, N // 2], I32, name="w2c", tag="big", align_bytes=64)
+        nc.sync.dma_start(out=w2c[:], in_=w2c_words.rearrange("e s p b -> p (e s) b").bitcast(I32))
+        gates = big.tile([P, TOP, T], F32, name="gates", tag="big", align_bytes=64)
+        nc.sync.dma_start(out=gates[:], in_=gate.rearrange("r p t -> p r t"))
+
+        h_words = [held([P, C], U32, f"h_words{e}") for e in range(E)]
+        h_bytes = [held([P, C], U8, f"h_bytes{e}") for e in range(E)]
+        for e, first, count, grouped in pieces:
+            nc.vector.quantize_mx(
+                out=h_words[e][:, first : first + count].bitcast(FP8X4),
+                scales=h_bytes[e][:, first : first + count],
+                in_=grouped[:],
+            )
+
+        def second_layer(bank_cols, e, b, first, count):
+            n_cols = slice(e % HOT * N + b * P, e % HOT * N + (b + 1) * P)
+            if e < HOT:
+                w_op = w2h[:, e, b * P : (b + 1) * P].bitcast(FP8X4)
+                w_scale = w1h_plane[W2H_ROW:P, n_cols]
+            else:
+                w_op = w2c[:, e - HOT, b * P // 2 : (b + 1) * P // 2].bitcast(FP4X4)
+                w_scale = w1h_plane[:, n_cols]
+            nc.tensor.matmul_mx(
+                out=bank_cols, lhsT=w_op, lhsT_scale=w_scale,
+                rhs=h_words[e][:, first : first + count].bitcast(FP8X4),
+                rhs_scale=h_bytes[e][:, first : first + count], start=True, stop=True,
+            )
+
+        y = [held([P, S], F32, f"y{b}") for b in range(N // P)]
+        for b in range(N // P):
+            for pair in range(E // 2):
+                bank = acc.tile([P, 2 * C], F32, name="acc")
+                base = pair * 2 * C
+                if b == 0 and pair == E // 2 - 1:
+                    second_layer(bank[:, 0:C], E - 2, b, 0, C)
+                    second_layer(bank[:, C : C + P], E - 1, b, 0, P)
+                    nc.scalar.copy(out=y[b][:, base : base + C + P], in_=bank[:, 0 : C + P])
+                    last = acc.tile([P, 2 * C], F32, name="acc")
+                    second_layer(last[:, 0:P], E - 1, b, P, P)
+                    nc.scalar.copy(out=y[b][:, S - P : S], in_=last[:, 0:P])
+                else:
+                    for i in range(2):
+                        second_layer(bank[:, i * C : (i + 1) * C], 2 * pair + i, b, 0, C)
+                    if b == 0 and pair == 0:
+                        nc.vector.tensor_copy(out=y[b][:, base : base + 2 * C], in_=bank[:])
+                    else:
+                        nc.scalar.copy(out=y[b][:, base : base + 2 * C], in_=bank[:])
+
+        for b in range(N // P):
+            prods = [held([P, T], F32, f"prod{b}_{r}") for r in range(TOP)]
+            res = held([P, T], F32, f"res{b}")
+            if b < N // P - 1:
+                for r in range(TOP):
+                    nc.vector.tensor_tensor(prods[r][:], y[b][:].indirect(pos[r][:]), gates[:, r, :], MULT)
+                summed = turn.tile([P, T], F32, name="turn")
+                for j in range(T // P):
+                    cols = slice(j * P, (j + 1) * P)
+                    for r in range(TOP):
+                        nc.tensor.matmul(
+                            summed[:, cols], lhsT=prods[r][:, cols], rhs=ident[:], is_transpose=True,
+                            start=(r == 0), stop=(r == TOP - 1),
+                        )
+                by_token = held([P, T], F32, f"by_token{b}")
+                nc.scalar.copy(out=by_token[:], in_=summed[:])
+                back = acc.tile([P, T], F32, name="acc")
+                for j in range(T // P):
+                    cols = slice(j * P, (j + 1) * P)
+                    nc.tensor.transpose(back[:, cols], by_token[:, cols], ident[:])
+                nc.scalar.copy(out=res[:], in_=back[:])
+            else:
+                part = held([P, T], F32, "part")
+                for r in range(TOP):
+                    nc.vector.tensor_tensor(prods[r][:], y[b][:].indirect(pos[r][:]), gates[:, r, :], MULT)
+                nc.vector.tensor_tensor(part[:], prods[0][:], prods[1][:], ADD)
+                nc.vector.tensor_tensor(res[:], part[:], prods[2][:], ADD)
+            nc.sync.dma_start(out=out[b * P : (b + 1) * P, :], in_=res[:])

@@ -35,137 +35,154 @@ def tile_moe_hot_mlp_relu_kernel(
     with ExitStack() as ctx:
         lists = ctx.enter_context(tc.tile_pool(name="lists", bufs=1))
         keep = ctx.enter_context(tc.tile_pool(name="keep", bufs=1))
-        big = ctx.enter_context(tc.tile_pool(name="big", bufs=4))
-        ring = ctx.enter_context(tc.tile_pool(name="ring", bufs=4))
-        acc = ctx.enter_context(tc.psum_pool(name="acc", bufs=5))
-        turn = ctx.enter_context(tc.psum_pool(name="turn", bufs=3))
+        big = ctx.enter_context(tc.tile_pool(name="big", bufs=1))
+        ring = ctx.enter_context(tc.tile_pool(name="ring", bufs=1))
+        psum = ctx.enter_context(tc.psum_pool(name="psum", bufs=1))
+
+        def bank_tile(tag):
+            return psum.tile([P, 4 * P], F32, name=tag)
 
         def held(shape, dtype, name):
             return keep.tile(shape, dtype, name=name, align_bytes=64)
 
-        def zeroed_plane(width, name):
+        def zeroed_plane(engine, width, name):
             plane = held([P, width], U8, name)
-            nc.vector.memset(plane[:].bitcast(I32), 0)
+            engine.memset(plane[:].bitcast(I32), 0)
             return plane
 
-        def load_scale_rows(plane, row, scales):
+        def load_scale_rows(queue, plane, row, scales):
             rows = scales.bitcast(I32).rearrange("e s b i -> b (e s) i")
             view = plane.bitcast(I32).rearrange("p (a i) -> p a i", i=H // 4)
             for q in range(4):
-                nc.sync.dma_start(out=view[32 * q + row : 32 * q + row + 4], in_=rows[4 * q : 4 * q + 4])
+                queue.dma_start(out=view[32 * q + row : 32 * q + row + 4], in_=rows[4 * q : 4 * q + 4])
 
-        x_plane = zeroed_plane(T, "x_plane")
-        w1h_plane = zeroed_plane(HOT * PASSES * H, "w1h_plane")
-        w1c_plane = zeroed_plane(COLD * PASSES * H, "w1c_plane")
-        cold_planes = [zeroed_plane(COLD * C, f"cold_plane{s}") for s in range(1, PASSES)]
+        x_plane = zeroed_plane(nc.gpsimd, T, "x_plane")
+        w1h_planes = [zeroed_plane(nc.gpsimd, PASSES * H, "w1h_plane_first"), zeroed_plane(nc.gpsimd, (HOT - 1) * PASSES * H, "w1h_plane_rest")]
+        w1c_plane = zeroed_plane(nc.vector, COLD * PASSES * H, "w1c_plane")
+        cold_planes = {
+            (first, s): zeroed_plane(nc.vector, count * C, f"cold_plane{first}_{s}")
+            for first, count in ((HOT, 1), (HOT + 1, 2))
+            for s in range(1, PASSES)
+        }
         ident = held([P, P], F32, "ident")
         make_identity(nc, ident[:])
 
         offsets = lists.tile([P, S // 16], U16, name="offsets")
         nc.sync.dma_start(offsets[:], offs)
-        x_win = [held([P, T], I32, f"x_win{s}") for s in range(PASSES)]
+        x_first = held([P, T], I32, "x_first")
+        x_rest = held([P, PASSES - 1, T], I32, "x_rest")
+        x_win = [x_first[:]] + [x_rest[:, s, :] for s in range(PASSES - 1)]
+        x_source = x_words.rearrange("s p t d -> p s (t d)").bitcast(I32)
 
-        def load_tokens(s):
-            nc.sync.dma_start(out=x_win[s][:], in_=x_words[s].rearrange("p t d -> p (t d)").bitcast(I32))
-
-        def w1_tile(e):
-            return big.tile([P, PASSES, H if e < HOT else H // 2], I32, name=f"w1_{e}", tag="big", align_bytes=64)
+        def load_x_scales(queue, q):
+            queue.dma_start(
+                out=x_plane[:].bitcast(I32)[32 * q : 32 * q + 4 * PASSES, :],
+                in_=x_scales.bitcast(I32)[:, 4 * q : 4 * q + 4, :],
+            )
 
         def w1_source(e):
             if e < HOT:
                 return w1h_words[e].rearrange("s p i d -> p s (i d)").bitcast(I32)
             return w1c_words[e - HOT].rearrange("s p b -> p s b").bitcast(I32)
 
-        for s in range(PASSES):
-            load_tokens(s)
-        w1 = [w1_tile(0)]
-        nc.sync.dma_start(out=w1[0][:, 0:1, :], in_=w1_source(0)[:, 0:1, :])
-        for q in range(4):
-            nc.sync.dma_start(
-                out=x_plane[:].bitcast(I32)[32 * q : 32 * q + 4 * PASSES, :],
-                in_=x_scales.bitcast(I32)[:, 4 * q : 4 * q + 4, :],
-            )
-        load_scale_rows(w1h_plane[:], W1H_ROW, w1h_scales)
-        nc.sync.dma_start(out=w1[0][:, 1:PASSES, :], in_=w1_source(0)[:, 1:PASSES, :])
+        w1 = {}
 
-        def load_w1(e):
-            w1.append(w1_tile(e))
-            nc.sync.dma_start(out=w1[e][:], in_=w1_source(e))
+        def load_w1(e, first, last, tag):
+            w = big.tile([P, last - first, H if e < HOT else H // 2], I32, name=f"w1_{e}_{first}", tag=tag, align_bytes=64)
+            nc.sync.dma_start(out=w[:], in_=w1_source(e)[:, first:last, :])
+            for s in range(first, last):
+                w1[e, s] = w[:, s - first, :]
 
-        load_w1(1)
-        load_scale_rows(w1c_plane[:], 0, w1c_scales)
-        load_w1(2)
-        load_w1(3)
+        load_x_scales(nc.scalar, 0)
+        nc.sync.dma_start(out=x_first[:], in_=x_source[:, 0, :])
+        load_x_scales(nc.scalar, 1)
+        load_w1(0, 0, 1, "w1_first")
+        load_x_scales(nc.sync, 2)
+        load_x_scales(nc.sync, 3)
+        nc.sync.dma_start(out=x_rest[:], in_=x_source[:, 1:PASSES, :])
+        load_scale_rows(nc.sync, w1h_planes[0][:], W1H_ROW, w1h_scales[0:1])
+        load_w1(0, 1, PASSES, "slot_a")
+        load_w1(1, 0, PASSES, "w1_1")
+        load_scale_rows(nc.sync, w1h_planes[1][:], W1H_ROW, w1h_scales[1:HOT])
+        load_w1(2, 0, PASSES, "w1_2")
+        load_scale_rows(nc.sync, w1c_plane[:], 0, w1c_scales)
+        load_w1(3, 0, PASSES, "w1_3")
 
         def slots_of(first, count):
             return offsets[:, first // 16 : (first + count) // 16]
 
+        w2c = big.tile([P, COLD, N // 2], I32, name="w2c", align_bytes=64)
+        w2h = big.tile([P, HOT, N], I32, name="w2h", align_bytes=64)
         tok_words = {}
         tok_bytes = {}
 
         def gather_words(e, s):
-            words = ring.tile([P, C], U32, name="tok", align_bytes=64)
+            words = ring.tile([P, C], U32, name=f"tok{(e * PASSES + s) % 6}", align_bytes=64)
             tok_words[e, s] = words
             step = P if (e, s) == (E - 1, PASSES - 1) else C
             for first in range(0, C, step):
                 nc.vector.tensor_copy(
                     words[:, first : first + step],
-                    x_win[s][:].bitcast(U32).indirect(slots_of(e * C + first, step)),
+                    x_win[s].bitcast(U32).indirect(slots_of(e * C + first, step)),
                 )
 
         def gather_bytes(e, tile, col):
             tok_bytes[e] = (tile, col)
             nc.vector.tensor_copy(tile[:, col : col + C], x_plane[:].indirect(slots_of(e * C, C)))
 
-        def byte_tile():
-            return ring.tile([P, 2 * C], U8, name="tok_bytes", bufs=2, align_bytes=64)
+        def byte_tile(e):
+            return ring.tile([P, 2 * C], U8, name=f"tok_bytes{e % 2}", align_bytes=64)
 
         def shift_rows(first, count):
             tile, col = tok_bytes[first]
-            dst = (first - HOT) * C
             for s in range(1, PASSES):
                 nc.sync.dma_start(
-                    out=cold_planes[s - 1][:, dst : dst + count * C].bitcast(I32)[0:SHIFT_ROWS, :],
+                    out=cold_planes[first, s][:].bitcast(I32)[0:SHIFT_ROWS, :],
                     in_=tile[:, col : col + count * C].bitcast(I32)[4 * s : 4 * s + SHIFT_ROWS, :],
                 )
 
         def gathers(e):
-            if e in (0, 1, 2, 4):
-                tile = byte_tile()
+            if e < HOT:
+                tile = byte_tile(e)
                 gather_bytes(e, tile, 0)
             gather_words(e, 0)
-            if e in (2, 4):
-                gather_bytes(e + 1, tile, C)
-                if e == 2:
-                    shift_rows(3, 1)
-                else:
-                    shift_rows(4, 2)
+            if e == HOT - 1:
+                gather_bytes(HOT, tile, C)
+                shift_rows(HOT, 1)
+                load_w1(HOT + 1, 0, PASSES, "w1_4")
             for s in range(1, PASSES):
                 gather_words(e, s)
+            if e == HOT - 1:
+                tile = big.tile([P, 2 * C], U8, name="late_bytes", tag="slot_a", align_bytes=64)
+                gather_bytes(HOT + 1, tile, 0)
+                gather_bytes(HOT + 2, tile, C)
+                shift_rows(HOT + 1, 2)
+                load_w1(E - 1, 0, PASSES, "w1_5")
+                nc.sync.dma_start(out=w2h[:], in_=w2h_words.rearrange("e s p n d -> p (e s) (n d)").bitcast(I32))
+                nc.sync.dma_start(out=w2c[:], in_=w2c_words.rearrange("e s p b -> p (e s) b").bitcast(I32))
 
-        pos = []
-        for r, src in enumerate((pos1, pos2, pos3)):
-            lst = lists.tile([P, T // 16], U16, name=f"pos{r}")
-            nc.sync.dma_start(lst[:], src)
-            pos.append(lst)
 
         def first_layer(e):
-            banks = [acc.tile([P, H], F32, name="acc") for j in range(2)]
-            for s in range(PASSES):
-                for j in range(2):
+            banks = [bank_tile(f"even{e % 3}"), bank_tile(f"odd{e % 2}")]
+            order = [(0, 0), (0, 1), (1, 0), (2, 0), (1, 1), (2, 1)]
+            if e == E - 1:
+                order = [(s, j) for s in range(PASSES) for j in range(2)]
+            for s, j in order:
+                if True:
                     cols = slice(j * P, (j + 1) * P)
                     w_cols = slice((e % HOT * PASSES + s) * H, (e % HOT * PASSES + s + 1) * H)
                     if e < HOT:
                         tok_scale = tok_bytes[e][0][4 * s : P, cols]
-                        w_op = w1[e][:, s, :].bitcast(FP8X4)
-                        w_scale = w1h_plane[W1H_ROW:P, w_cols]
+                        w_op = w1[e, s].bitcast(FP8X4)
+                        first = (max(e - 1, 0) * PASSES + s) * H
+                        w_scale = w1h_planes[min(e, 1)][W1H_ROW:P, first : first + H]
                     else:
                         if s == 0:
                             plane, first = tok_bytes[e]
                         else:
-                            plane, first = cold_planes[s - 1], (e - HOT) * C
+                            plane, first = cold_planes[min(e, HOT + 1), s], max(e - HOT - 1, 0) * C
                         tok_scale = plane[:, first + j * P : first + (j + 1) * P]
-                        w_op = w1[e][:, s, :].bitcast(FP4X4)
+                        w_op = w1[e, s].bitcast(FP4X4)
                         w_scale = w1c_plane[:, w_cols]
                     nc.tensor.matmul_mx(
                         out=banks[j][:], lhsT=tok_words[e, s][:, cols].bitcast(FP8X4), lhsT_scale=tok_scale,
@@ -174,52 +191,55 @@ def tile_moe_hot_mlp_relu_kernel(
             hidden = []
             for j in range(2):
                 hb = held([P, H], BF16, f"hb{e}_{j}")
-                nc.scalar.activation(
-                    out=hb[:].rearrange("t (u p d) -> t u p d", u=2, d=2),
-                    in_=banks[j][:].rearrange("t (p u d) -> t u p d", u=2, d=2),
-                    func=RELU,
-                )
+                laid = hb[:].rearrange("t (u p d) -> t u p d", u=2, d=2)
+                sums = banks[j][:].rearrange("t (p u d) -> t u p d", u=2, d=2)
+                if (e, j) == (E - 1, 1):
+                    nc.vector.tensor_scalar_max(laid, sums, 0.0)
+                else:
+                    nc.scalar.activation(out=laid, in_=sums, func=RELU)
                 hidden.append(hb)
             return hidden
 
-        def turn_hidden(tiles, name):
+        def turn_hidden(tiles, name, tag, copy):
             n = len(tiles)
-            bank = turn.tile([P, 4 * P], F32, name="turn")
+            bank = bank_tile(tag)
             for j, hb in enumerate(tiles):
                 words = hb[:].bitcast(F32)
                 for u in range(2):
                     col = (2 * j + u) * P
                     nc.tensor.transpose(bank[:, col : col + P], words[:, u * P : (u + 1) * P], ident[:])
             grouped = held([P, n * H], BF16, name)
-            nc.scalar.copy(
+            copy(
                 out=grouped[:].bitcast(F32).rearrange("p (j t u) -> p j t u", j=n, u=2),
                 in_=bank[:, 0 : 2 * n * P].rearrange("p (j u t) -> p j t u", j=n, u=2),
             )
             return grouped
 
+        w2_plane = w1h_planes[1][:, PASSES * H : 2 * PASSES * H]
         pieces = []
         pending = None
         for e in range(E):
             gathers(e)
             hidden = first_layer(e)
-            if e + 4 < E:
-                load_w1(e + 4)
-            if e == 0:
-                w2_plane = w1h_plane[:, 0 : HOT * N]
-                load_scale_rows(w2_plane, W2H_ROW, w2h_scales)
-                load_scale_rows(w2_plane, 0, w2c_scales)
-            if pending is not None:
-                pieces.append((e - 1, 0, C, turn_hidden(pending, f"grouped{e - 1}")))
-            pending = hidden
-        for j in range(2):
-            pieces.append((E - 1, j * P, P, turn_hidden(pending[j : j + 1], f"grouped_last{j}")))
+            if e == HOT - 1:
+                load_scale_rows(nc.sync, w2_plane[:], W2H_ROW, w2h_scales)
+                load_scale_rows(nc.sync, w2_plane[:], 0, w2c_scales)
+            if 0 < e < E - 1:
+                pieces.append((e - 1, 0, C, turn_hidden(pending, f"grouped{e - 1}", f"even{e % 3}", nc.scalar.copy)))
+            if e < E - 1:
+                pending = hidden
+        pieces.append((E - 1, 0, P, turn_hidden(hidden[0:1], "grouped_a", "spare0", nc.scalar.copy)))
+        pieces.append((E - 2, 0, C, turn_hidden(pending, "grouped_4", "even2", nc.vector.tensor_copy)))
+        pieces.append((E - 1, P, P, turn_hidden(hidden[1:2], "grouped_b", "spare1", nc.scalar.copy)))
 
-        w2h = big.tile([P, HOT, N], I32, name="w2h", tag="big", align_bytes=64)
-        nc.sync.dma_start(out=w2h[:], in_=w2h_words.rearrange("e s p n d -> p (e s) (n d)").bitcast(I32))
-        w2c = big.tile([P, COLD, N // 2], I32, name="w2c", tag="big", align_bytes=64)
-        nc.sync.dma_start(out=w2c[:], in_=w2c_words.rearrange("e s p b -> p (e s) b").bitcast(I32))
-        gates = big.tile([P, TOP, T], F32, name="gates", tag="big", align_bytes=64)
+        pos = []
+        for r, src in enumerate((pos1, pos2, pos3)):
+            lst = lists.tile([P, T // 16], U16, name=f"pos{r}")
+            nc.sync.dma_start(lst[:], src)
+            pos.append(lst)
+        gates = big.tile([P, TOP, T], F32, name="gates", align_bytes=64)
         nc.sync.dma_start(out=gates[:], in_=gate.rearrange("r p t -> p r t"))
+
 
         h_words = [held([P, C], U32, f"h_words{e}") for e in range(E)]
         h_bytes = [held([P, C], U8, f"h_bytes{e}") for e in range(E)]
@@ -234,10 +254,10 @@ def tile_moe_hot_mlp_relu_kernel(
             n_cols = slice(e % HOT * N + b * P, e % HOT * N + (b + 1) * P)
             if e < HOT:
                 w_op = w2h[:, e, b * P : (b + 1) * P].bitcast(FP8X4)
-                w_scale = w1h_plane[W2H_ROW:P, n_cols]
+                w_scale = w2_plane[W2H_ROW:P, n_cols]
             else:
                 w_op = w2c[:, e - HOT, b * P // 2 : (b + 1) * P // 2].bitcast(FP4X4)
-                w_scale = w1h_plane[:, n_cols]
+                w_scale = w2_plane[:, n_cols]
             nc.tensor.matmul_mx(
                 out=bank_cols, lhsT=w_op, lhsT_scale=w_scale,
                 rhs=h_words[e][:, first : first + count].bitcast(FP8X4),
@@ -245,21 +265,25 @@ def tile_moe_hot_mlp_relu_kernel(
             )
 
         y = [held([P, S], F32, f"y{b}") for b in range(N // P)]
+        y_tags = ["spare2", "even0", "even1", "odd0"]
+        y_count = 0
         for b in range(N // P):
             for pair in range(E // 2):
-                bank = acc.tile([P, 2 * C], F32, name="acc")
+                bank = bank_tile(y_tags[y_count % 4])
+                y_count = y_count + 1
                 base = pair * 2 * C
                 if b == 0 and pair == E // 2 - 1:
                     second_layer(bank[:, 0:C], E - 2, b, 0, C)
                     second_layer(bank[:, C : C + P], E - 1, b, 0, P)
                     nc.scalar.copy(out=y[b][:, base : base + C + P], in_=bank[:, 0 : C + P])
-                    last = acc.tile([P, 2 * C], F32, name="acc")
+                    last = bank_tile(y_tags[y_count % 4])
+                    y_count = y_count + 1
                     second_layer(last[:, 0:P], E - 1, b, P, P)
-                    nc.scalar.copy(out=y[b][:, S - P : S], in_=last[:, 0:P])
+                    nc.vector.tensor_copy(out=y[b][:, S - P : S], in_=last[:, 0:P])
                 else:
                     for i in range(2):
                         second_layer(bank[:, i * C : (i + 1) * C], 2 * pair + i, b, 0, C)
-                    if b == 0 and pair == 0:
+                    if b == 0 and pair == 1:
                         nc.vector.tensor_copy(out=y[b][:, base : base + 2 * C], in_=bank[:])
                     else:
                         nc.scalar.copy(out=y[b][:, base : base + 2 * C], in_=bank[:])
@@ -270,7 +294,7 @@ def tile_moe_hot_mlp_relu_kernel(
             if b < N // P - 1:
                 for r in range(TOP):
                     nc.vector.tensor_tensor(prods[r][:], y[b][:].indirect(pos[r][:]), gates[:, r, :], MULT)
-                summed = turn.tile([P, T], F32, name="turn")
+                summed = bank_tile(("odd1", "spare0")[b % 2])
                 for j in range(T // P):
                     cols = slice(j * P, (j + 1) * P)
                     for r in range(TOP):
@@ -280,15 +304,23 @@ def tile_moe_hot_mlp_relu_kernel(
                         )
                 by_token = held([P, T], F32, f"by_token{b}")
                 nc.scalar.copy(out=by_token[:], in_=summed[:])
-                back = acc.tile([P, T], F32, name="acc")
+                back = bank_tile(("even2", "spare1")[b % 2])
                 for j in range(T // P):
                     cols = slice(j * P, (j + 1) * P)
                     nc.tensor.transpose(back[:, cols], by_token[:, cols], ident[:])
                 nc.scalar.copy(out=res[:], in_=back[:])
+                nc.scalar.dma_start(out=out[b * P : (b + 1) * P, :], in_=res[:])
             else:
                 part = held([P, T], F32, "part")
-                for r in range(TOP):
+                for r in range(TOP - 1):
                     nc.vector.tensor_tensor(prods[r][:], y[b][:].indirect(pos[r][:]), gates[:, r, :], MULT)
                 nc.vector.tensor_tensor(part[:], prods[0][:], prods[1][:], ADD)
-                nc.vector.tensor_tensor(res[:], part[:], prods[2][:], ADD)
-            nc.sync.dma_start(out=out[b * P : (b + 1) * P, :], in_=res[:])
+                half = T // 2
+                for i in range(2):
+                    cols = slice(i * half, (i + 1) * half)
+                    window = y[b][:].indirect(pos[TOP - 1][:, i * half // 16 : (i + 1) * half // 16])
+                    nc.vector.tensor_tensor(prods[TOP - 1][:, cols], window, gates[:, TOP - 1, cols], MULT)
+                for i in range(2):
+                    cols = slice(i * half, (i + 1) * half)
+                    nc.vector.tensor_tensor(res[:, cols], part[:, cols], prods[TOP - 1][:, cols], ADD)
+                    nc.sync.dma_start(out=out[b * P : (b + 1) * P, cols], in_=res[:, cols])

@@ -57,7 +57,10 @@ def tile_moe_hot_mlp_relu_kernel(
                 queue.dma_start(out=view[32 * q + row : 32 * q + row + 4], in_=rows[4 * q : 4 * q + 4])
 
         x_plane = zeroed_plane(nc.gpsimd, T, "x_plane")
-        w1h_planes = [zeroed_plane(nc.gpsimd, PASSES * H, "w1h_plane_first"), zeroed_plane(nc.gpsimd, (HOT - 1) * PASSES * H, "w1h_plane_rest")]
+        w1h_plane = held([P, HOT * PASSES * H], U8, "w1h_plane")
+        half_plane = HOT * PASSES * H // 2
+        nc.gpsimd.memset(w1h_plane[:, 0:half_plane].bitcast(I32), 0)
+        nc.vector.memset(w1h_plane[:, half_plane:].bitcast(I32), 0)
         w1c_plane = zeroed_plane(nc.vector, COLD * PASSES * H, "w1c_plane")
         cold_planes = {
             (first, s): zeroed_plane(nc.vector, count * C, f"cold_plane{first}_{s}")
@@ -100,26 +103,28 @@ def tile_moe_hot_mlp_relu_kernel(
         load_x_scales(nc.sync, 2)
         load_x_scales(nc.sync, 3)
         nc.sync.dma_start(out=x_rest[:], in_=x_source[:, 1:PASSES, :])
-        load_scale_rows(nc.sync, w1h_planes[0][:], W1H_ROW, w1h_scales[0:1])
+        load_scale_rows(nc.sync, w1h_plane[:], W1H_ROW, w1h_scales)
         load_w1(0, 1, PASSES, "slot_a")
         load_w1(1, 0, PASSES, "w1_1")
-        load_scale_rows(nc.sync, w1h_planes[1][:], W1H_ROW, w1h_scales[1:HOT])
         load_w1(2, 0, PASSES, "w1_2")
         load_scale_rows(nc.sync, w1c_plane[:], 0, w1c_scales)
         load_w1(3, 0, PASSES, "w1_3")
+        load_w1(4, 0, PASSES, "w1_4")
 
         def slots_of(first, count):
             return offsets[:, first // 16 : (first + count) // 16]
 
-        w2c = big.tile([P, COLD, N // 2], I32, name="w2c", align_bytes=64)
-        w2h = big.tile([P, HOT, N], I32, name="w2h", align_bytes=64)
         tok_words = {}
         tok_bytes = {}
 
-        def gather_words(e, s):
-            words = ring.tile([P, C], U32, name=f"tok{(e * PASSES + s) % 6}", align_bytes=64)
+        def pass_order(e):
+            return (1, 2, 0) if e > HOT else (0, 1, 2)
+
+        def gather_words(e, i):
+            s = pass_order(e)[i]
+            words = ring.tile([P, C], U32, name=f"tok{(e * PASSES + i) % 6}", align_bytes=64)
             tok_words[e, s] = words
-            step = P if (e, s) == (E - 1, PASSES - 1) else C
+            step = P if (e, i) == (E - 1, PASSES - 1) else C
             for first in range(0, C, step):
                 nc.vector.tensor_copy(
                     words[:, first : first + step],
@@ -149,7 +154,6 @@ def tile_moe_hot_mlp_relu_kernel(
             if e == HOT - 1:
                 gather_bytes(HOT, tile, C)
                 shift_rows(HOT, 1)
-                load_w1(HOT + 1, 0, PASSES, "w1_4")
             for s in range(1, PASSES):
                 gather_words(e, s)
             if e == HOT - 1:
@@ -157,16 +161,14 @@ def tile_moe_hot_mlp_relu_kernel(
                 gather_bytes(HOT + 1, tile, 0)
                 gather_bytes(HOT + 2, tile, C)
                 shift_rows(HOT + 1, 2)
-                load_w1(E - 1, 0, PASSES, "w1_5")
-                nc.sync.dma_start(out=w2h[:], in_=w2h_words.rearrange("e s p n d -> p (e s) (n d)").bitcast(I32))
-                nc.sync.dma_start(out=w2c[:], in_=w2c_words.rearrange("e s p b -> p (e s) b").bitcast(I32))
+                load_w1(E - 1, 0, PASSES, "w1_1")
 
 
         def first_layer(e):
             banks = [bank_tile(f"even{e % 3}"), bank_tile(f"odd{e % 2}")]
-            order = [(0, 0), (0, 1), (1, 0), (2, 0), (1, 1), (2, 1)]
+            order = [(s, j) for j in range(2) for s in pass_order(e)]
             if e == E - 1:
-                order = [(s, j) for s in range(PASSES) for j in range(2)]
+                order = [(s, j) for s in pass_order(e) for j in range(2)]
             for s, j in order:
                 if True:
                     cols = slice(j * P, (j + 1) * P)
@@ -174,8 +176,7 @@ def tile_moe_hot_mlp_relu_kernel(
                     if e < HOT:
                         tok_scale = tok_bytes[e][0][4 * s : P, cols]
                         w_op = w1[e, s].bitcast(FP8X4)
-                        first = (max(e - 1, 0) * PASSES + s) * H
-                        w_scale = w1h_planes[min(e, 1)][W1H_ROW:P, first : first + H]
+                        w_scale = w1h_plane[W1H_ROW:P, w_cols]
                     else:
                         if s == 0:
                             plane, first = tok_bytes[e]
@@ -186,7 +187,7 @@ def tile_moe_hot_mlp_relu_kernel(
                         w_scale = w1c_plane[:, w_cols]
                     nc.tensor.matmul_mx(
                         out=banks[j][:], lhsT=tok_words[e, s][:, cols].bitcast(FP8X4), lhsT_scale=tok_scale,
-                        rhs=w_op, rhs_scale=w_scale, start=(s == 0), stop=(s == PASSES - 1),
+                        rhs=w_op, rhs_scale=w_scale, start=(s == pass_order(e)[0]), stop=(s == pass_order(e)[-1]),
                     )
             hidden = []
             for j in range(2):
@@ -215,13 +216,17 @@ def tile_moe_hot_mlp_relu_kernel(
             )
             return grouped
 
-        w2_plane = w1h_planes[1][:, PASSES * H : 2 * PASSES * H]
+        w2_plane = w1h_plane[:, 2 * PASSES * H : 3 * PASSES * H]
         pieces = []
         pending = None
         for e in range(E):
             gathers(e)
             hidden = first_layer(e)
             if e == HOT - 1:
+                w2h = ring.tile([P, HOT, N], I32, name="w2h", tag="tok_bytes1", align_bytes=64)
+                nc.sync.dma_start(out=w2h[:], in_=w2h_words.rearrange("e s p n d -> p (e s) (n d)").bitcast(I32))
+                w2c = big.tile([P, COLD, N // 2], I32, name="w2c", tag="w1_2", align_bytes=64)
+                nc.sync.dma_start(out=w2c[:], in_=w2c_words.rearrange("e s p b -> p (e s) b").bitcast(I32))
                 load_scale_rows(nc.sync, w2_plane[:], W2H_ROW, w2h_scales)
                 load_scale_rows(nc.sync, w2_plane[:], 0, w2c_scales)
             if 0 < e < E - 1:
@@ -237,7 +242,7 @@ def tile_moe_hot_mlp_relu_kernel(
             lst = lists.tile([P, T // 16], U16, name=f"pos{r}")
             nc.sync.dma_start(lst[:], src)
             pos.append(lst)
-        gates = big.tile([P, TOP, T], F32, name="gates", align_bytes=64)
+        gates = big.tile([P, TOP, T], F32, name="gates", tag="w1_3", align_bytes=64)
         nc.sync.dma_start(out=gates[:], in_=gate.rearrange("r p t -> p r t"))
 
 
@@ -283,10 +288,7 @@ def tile_moe_hot_mlp_relu_kernel(
                 else:
                     for i in range(2):
                         second_layer(bank[:, i * C : (i + 1) * C], 2 * pair + i, b, 0, C)
-                    if b == 0 and pair == 1:
-                        nc.vector.tensor_copy(out=y[b][:, base : base + 2 * C], in_=bank[:])
-                    else:
-                        nc.scalar.copy(out=y[b][:, base : base + 2 * C], in_=bank[:])
+                    nc.scalar.copy(out=y[b][:, base : base + 2 * C], in_=bank[:])
 
         for b in range(N // P):
             prods = [held([P, T], F32, f"prod{b}_{r}") for r in range(TOP)]
@@ -294,16 +296,25 @@ def tile_moe_hot_mlp_relu_kernel(
             if b < N // P - 1:
                 for r in range(TOP):
                     nc.vector.tensor_tensor(prods[r][:], y[b][:].indirect(pos[r][:]), gates[:, r, :], MULT)
-                summed = bank_tile(("odd1", "spare0")[b % 2])
-                for j in range(T // P):
-                    cols = slice(j * P, (j + 1) * P)
-                    for r in range(TOP):
-                        nc.tensor.matmul(
-                            summed[:, cols], lhsT=prods[r][:, cols], rhs=ident[:], is_transpose=True,
-                            start=(r == 0), stop=(r == TOP - 1),
-                        )
                 by_token = held([P, T], F32, f"by_token{b}")
-                nc.scalar.copy(out=by_token[:], in_=summed[:])
+                tiles = [slice(j * P, (j + 1) * P) for j in range(T // P)]
+                if b < N // P - 2:
+                    summed = bank_tile(("odd1", "spare0")[b])
+                    sums = [summed[:, cols] for cols in tiles]
+                    order = [(j, r) for j in range(T // P) for r in range(TOP)]
+                else:
+                    sums = [bank_tile(tag)[:, 0:P] for tag in y_tags]
+                    order = [(j, r) for r in range(TOP) for j in range(T // P)]
+                for j, r in order:
+                    nc.tensor.matmul(
+                        sums[j], lhsT=prods[r][:, tiles[j]], rhs=ident[:], is_transpose=True,
+                        start=(r == 0), stop=(r == TOP - 1),
+                    )
+                if b < N // P - 2:
+                    nc.scalar.copy(out=by_token[:], in_=summed[:])
+                else:
+                    for j in range(T // P):
+                        nc.scalar.copy(out=by_token[:, tiles[j]], in_=sums[j])
                 back = bank_tile(("even2", "spare1")[b % 2])
                 for j in range(T // P):
                     cols = slice(j * P, (j + 1) * P)

@@ -8,7 +8,12 @@ COLD = E - HOT
 S = E * C
 P = 128
 PASSES = K // 512
+BLOCKS = N // P
 FLOPS = 2 * S * (K * H + H * N)
+BYTES = (
+    K * T * 33 // 32 + HOT * (K * H + H * N) * 33 // 32 + COLD * (K * H + H * N) * 17 // 32
+    + 4 * TOP * T + 2 * P * (S + TOP * T) // 16 + 4 * N * T
+)
 
 F32 = mybir.dt.float32
 BF16 = mybir.dt.bfloat16
@@ -25,6 +30,7 @@ ADD = mybir.AluOpType.add
 W1H_ROW = 4
 W2H_ROW = 8
 SHIFT_ROWS = 112
+WORD_RING = 2 * PASSES
 
 
 def tile_moe_hot_mlp_relu_kernel(
@@ -50,11 +56,11 @@ def tile_moe_hot_mlp_relu_kernel(
             engine.memset(plane[:].bitcast(I32), 0)
             return plane
 
-        def load_scale_rows(queue, plane, row, scales):
+        def load_scale_rows(plane, row, scales):
             rows = scales.bitcast(I32).rearrange("e s b i -> b (e s) i")
             view = plane.bitcast(I32).rearrange("p (a i) -> p a i", i=H // 4)
-            for q in range(4):
-                queue.dma_start(out=view[32 * q + row : 32 * q + row + 4], in_=rows[4 * q : 4 * q + 4])
+            for r in range(4):
+                nc.sync.dma_start(out=view[row + r : P : 32], in_=rows[r:16:4])
 
         x_plane = zeroed_plane(nc.gpsimd, T, "x_plane")
         w1h_plane = held([P, HOT * PASSES * H], U8, "w1h_plane")
@@ -64,7 +70,7 @@ def tile_moe_hot_mlp_relu_kernel(
         w1c_plane = zeroed_plane(nc.vector, COLD * PASSES * H, "w1c_plane")
         cold_planes = {
             (first, s): zeroed_plane(nc.vector, count * C, f"cold_plane{first}_{s}")
-            for first, count in ((HOT, 1), (HOT + 1, 2))
+            for first, count in ((HOT, 1), (HOT + 1, COLD - 1))
             for s in range(1, PASSES)
         }
         ident = held([P, P], F32, "ident")
@@ -91,7 +97,8 @@ def tile_moe_hot_mlp_relu_kernel(
         w1 = {}
 
         def load_w1(e, first, last, tag):
-            w = big.tile([P, last - first, H if e < HOT else H // 2], I32, name=f"w1_{e}_{first}", tag=tag, align_bytes=64)
+            width = H if e < HOT else H // 2
+            w = big.tile([P, last - first, width], I32, name=f"w1_{e}_{first}", tag=tag, align_bytes=64)
             nc.sync.dma_start(out=w[:], in_=w1_source(e)[:, first:last, :])
             for s in range(first, last):
                 w1[e, s] = w[:, s - first, :]
@@ -99,15 +106,15 @@ def tile_moe_hot_mlp_relu_kernel(
         load_x_scales(nc.scalar, 0)
         nc.sync.dma_start(out=x_first[:], in_=x_source[:, 0, :])
         load_x_scales(nc.scalar, 1)
-        load_w1(0, 0, 1, "w1_first")
+        load_w1(0, 0, 1, "w1_0_first")
         load_x_scales(nc.sync, 2)
         load_x_scales(nc.sync, 3)
         nc.sync.dma_start(out=x_rest[:], in_=x_source[:, 1:PASSES, :])
-        load_scale_rows(nc.sync, w1h_plane[:], W1H_ROW, w1h_scales)
-        load_w1(0, 1, PASSES, "slot_a")
+        load_scale_rows(w1h_plane[:], W1H_ROW, w1h_scales)
+        load_w1(0, 1, PASSES, "w1_0_rest")
         load_w1(1, 0, PASSES, "w1_1")
         load_w1(2, 0, PASSES, "w1_2")
-        load_scale_rows(nc.sync, w1c_plane[:], 0, w1c_scales)
+        load_scale_rows(w1c_plane[:], 0, w1c_scales)
         load_w1(3, 0, PASSES, "w1_3")
         load_w1(4, 0, PASSES, "w1_4")
 
@@ -122,7 +129,7 @@ def tile_moe_hot_mlp_relu_kernel(
 
         def gather_words(e, i):
             s = pass_order(e)[i]
-            words = ring.tile([P, C], U32, name=f"tok{(e * PASSES + i) % 6}", align_bytes=64)
+            words = ring.tile([P, C], U32, name=f"tok{(e * PASSES + i) % WORD_RING}", align_bytes=64)
             tok_words[e, s] = words
             step = P if (e, i) == (E - 1, PASSES - 1) else C
             for first in range(0, C, step):
@@ -135,9 +142,6 @@ def tile_moe_hot_mlp_relu_kernel(
             tok_bytes[e] = (tile, col)
             nc.vector.tensor_copy(tile[:, col : col + C], x_plane[:].indirect(slots_of(e * C, C)))
 
-        def byte_tile(e):
-            return ring.tile([P, 2 * C], U8, name=f"tok_bytes{e % 2}", align_bytes=64)
-
         def shift_rows(first, count):
             tile, col = tok_bytes[first]
             for s in range(1, PASSES):
@@ -148,47 +152,46 @@ def tile_moe_hot_mlp_relu_kernel(
 
         def gathers(e):
             if e < HOT:
-                tile = byte_tile(e)
+                tile = ring.tile([P, 2 * C], U8, name=f"tok_bytes{e % 2}", align_bytes=64)
                 gather_bytes(e, tile, 0)
             gather_words(e, 0)
             if e == HOT - 1:
                 gather_bytes(HOT, tile, C)
                 shift_rows(HOT, 1)
-            for s in range(1, PASSES):
-                gather_words(e, s)
+            for i in range(1, PASSES):
+                gather_words(e, i)
             if e == HOT - 1:
-                tile = big.tile([P, 2 * C], U8, name="late_bytes", tag="slot_a", align_bytes=64)
-                gather_bytes(HOT + 1, tile, 0)
-                gather_bytes(HOT + 2, tile, C)
-                shift_rows(HOT + 1, 2)
+                late = big.tile([P, 2 * C], U8, name="late_bytes", tag="w1_0_rest", align_bytes=64)
+                gather_bytes(HOT + 1, late, 0)
+                gather_bytes(HOT + 2, late, C)
+                shift_rows(HOT + 1, COLD - 1)
                 load_w1(E - 1, 0, PASSES, "w1_1")
-
 
         def first_layer(e):
             banks = [bank_tile(f"even{e % 3}"), bank_tile(f"odd{e % 2}")]
-            order = [(s, j) for j in range(2) for s in pass_order(e)]
-            if e == E - 1:
+            if e < E - 1:
+                order = [(s, j) for j in range(2) for s in pass_order(e)]
+            else:
                 order = [(s, j) for s in pass_order(e) for j in range(2)]
             for s, j in order:
-                if True:
-                    cols = slice(j * P, (j + 1) * P)
-                    w_cols = slice((e % HOT * PASSES + s) * H, (e % HOT * PASSES + s + 1) * H)
-                    if e < HOT:
-                        tok_scale = tok_bytes[e][0][4 * s : P, cols]
-                        w_op = w1[e, s].bitcast(FP8X4)
-                        w_scale = w1h_plane[W1H_ROW:P, w_cols]
+                cols = slice(j * P, (j + 1) * P)
+                w_cols = slice((e % HOT * PASSES + s) * H, (e % HOT * PASSES + s + 1) * H)
+                if e < HOT:
+                    tok_scale = tok_bytes[e][0][4 * s : P, cols]
+                    w_op = w1[e, s].bitcast(FP8X4)
+                    w_scale = w1h_plane[W1H_ROW:P, w_cols]
+                else:
+                    if s == 0:
+                        plane, col = tok_bytes[e]
                     else:
-                        if s == 0:
-                            plane, first = tok_bytes[e]
-                        else:
-                            plane, first = cold_planes[min(e, HOT + 1), s], max(e - HOT - 1, 0) * C
-                        tok_scale = plane[:, first + j * P : first + (j + 1) * P]
-                        w_op = w1[e, s].bitcast(FP4X4)
-                        w_scale = w1c_plane[:, w_cols]
-                    nc.tensor.matmul_mx(
-                        out=banks[j][:], lhsT=tok_words[e, s][:, cols].bitcast(FP8X4), lhsT_scale=tok_scale,
-                        rhs=w_op, rhs_scale=w_scale, start=(s == pass_order(e)[0]), stop=(s == pass_order(e)[-1]),
-                    )
+                        plane, col = cold_planes[min(e, HOT + 1), s], max(e - HOT - 1, 0) * C
+                    tok_scale = plane[:, col + j * P : col + (j + 1) * P]
+                    w_op = w1[e, s].bitcast(FP4X4)
+                    w_scale = w1c_plane[:, w_cols]
+                nc.tensor.matmul_mx(
+                    out=banks[j][:], lhsT=tok_words[e, s][:, cols].bitcast(FP8X4), lhsT_scale=tok_scale,
+                    rhs=w_op, rhs_scale=w_scale, start=(s == pass_order(e)[0]), stop=(s == pass_order(e)[-1]),
+                )
             hidden = []
             for j in range(2):
                 hb = held([P, H], BF16, f"hb{e}_{j}")
@@ -205,10 +208,10 @@ def tile_moe_hot_mlp_relu_kernel(
             n = len(tiles)
             bank = bank_tile(tag)
             for j, hb in enumerate(tiles):
-                words = hb[:].bitcast(F32)
+                pairs = hb[:].bitcast(F32)
                 for u in range(2):
                     col = (2 * j + u) * P
-                    nc.tensor.transpose(bank[:, col : col + P], words[:, u * P : (u + 1) * P], ident[:])
+                    nc.tensor.transpose(bank[:, col : col + P], pairs[:, u * P : (u + 1) * P], ident[:])
             grouped = held([P, n * H], BF16, name)
             copy(
                 out=grouped[:].bitcast(F32).rearrange("p (j t u) -> p j t u", j=n, u=2),
@@ -216,26 +219,25 @@ def tile_moe_hot_mlp_relu_kernel(
             )
             return grouped
 
-        w2_plane = w1h_plane[:, 2 * PASSES * H : 3 * PASSES * H]
+        w2_plane = w1h_plane[:, (HOT - 1) * PASSES * H : HOT * PASSES * H]
         pieces = []
-        pending = None
+        hidden = []
         for e in range(E):
             gathers(e)
-            hidden = first_layer(e)
+            hidden.append(first_layer(e))
             if e == HOT - 1:
                 w2h = ring.tile([P, HOT, N], I32, name="w2h", tag="tok_bytes1", align_bytes=64)
                 nc.sync.dma_start(out=w2h[:], in_=w2h_words.rearrange("e s p n d -> p (e s) (n d)").bitcast(I32))
                 w2c = big.tile([P, COLD, N // 2], I32, name="w2c", tag="w1_2", align_bytes=64)
                 nc.sync.dma_start(out=w2c[:], in_=w2c_words.rearrange("e s p b -> p (e s) b").bitcast(I32))
-                load_scale_rows(nc.sync, w2_plane[:], W2H_ROW, w2h_scales)
-                load_scale_rows(nc.sync, w2_plane[:], 0, w2c_scales)
+                load_scale_rows(w2_plane[:], W2H_ROW, w2h_scales)
+                load_scale_rows(w2_plane[:], 0, w2c_scales)
             if 0 < e < E - 1:
-                pieces.append((e - 1, 0, C, turn_hidden(pending, f"grouped{e - 1}", f"even{e % 3}", nc.scalar.copy)))
-            if e < E - 1:
-                pending = hidden
-        pieces.append((E - 1, 0, P, turn_hidden(hidden[0:1], "grouped_a", "spare0", nc.scalar.copy)))
-        pieces.append((E - 2, 0, C, turn_hidden(pending, "grouped_4", "even2", nc.vector.tensor_copy)))
-        pieces.append((E - 1, P, P, turn_hidden(hidden[1:2], "grouped_b", "spare1", nc.scalar.copy)))
+                grouped = turn_hidden(hidden[e - 1], f"grouped{e - 1}", f"even{e % 3}", nc.scalar.copy)
+                pieces.append((e - 1, 0, C, grouped))
+        pieces.append((E - 1, 0, P, turn_hidden(hidden[E - 1][0:1], "grouped_a", "spare0", nc.scalar.copy)))
+        pieces.append((E - 2, 0, C, turn_hidden(hidden[E - 2], "grouped_4", "even2", nc.vector.tensor_copy)))
+        pieces.append((E - 1, P, P, turn_hidden(hidden[E - 1][1:2], "grouped_b", "spare1", nc.scalar.copy)))
 
         pos = []
         for r, src in enumerate((pos1, pos2, pos3)):
@@ -244,7 +246,6 @@ def tile_moe_hot_mlp_relu_kernel(
             pos.append(lst)
         gates = big.tile([P, TOP, T], F32, name="gates", tag="w1_3", align_bytes=64)
         nc.sync.dma_start(out=gates[:], in_=gate.rearrange("r p t -> p r t"))
-
 
         h_words = [held([P, C], U32, f"h_words{e}") for e in range(E)]
         h_bytes = [held([P, C], U8, f"h_bytes{e}") for e in range(E)]
@@ -269,20 +270,20 @@ def tile_moe_hot_mlp_relu_kernel(
                 rhs_scale=h_bytes[e][:, first : first + count], start=True, stop=True,
             )
 
-        y = [held([P, S], F32, f"y{b}") for b in range(N // P)]
+        y = [held([P, S], F32, f"y{b}") for b in range(BLOCKS)]
         y_tags = ["spare2", "even0", "even1", "odd0"]
-        y_count = 0
-        for b in range(N // P):
+        turn = 0
+        for b in range(BLOCKS):
             for pair in range(E // 2):
-                bank = bank_tile(y_tags[y_count % 4])
-                y_count = y_count + 1
+                bank = bank_tile(y_tags[turn % len(y_tags)])
+                turn = turn + 1
                 base = pair * 2 * C
                 if b == 0 and pair == E // 2 - 1:
                     second_layer(bank[:, 0:C], E - 2, b, 0, C)
                     second_layer(bank[:, C : C + P], E - 1, b, 0, P)
                     nc.scalar.copy(out=y[b][:, base : base + C + P], in_=bank[:, 0 : C + P])
-                    last = bank_tile(y_tags[y_count % 4])
-                    y_count = y_count + 1
+                    last = bank_tile(y_tags[turn % len(y_tags)])
+                    turn = turn + 1
                     second_layer(last[:, 0:P], E - 1, b, P, P)
                     nc.vector.tensor_copy(out=y[b][:, S - P : S], in_=last[:, 0:P])
                 else:
@@ -290,34 +291,34 @@ def tile_moe_hot_mlp_relu_kernel(
                         second_layer(bank[:, i * C : (i + 1) * C], 2 * pair + i, b, 0, C)
                     nc.scalar.copy(out=y[b][:, base : base + 2 * C], in_=bank[:])
 
-        for b in range(N // P):
+        token_tiles = [slice(j * P, (j + 1) * P) for j in range(T // P)]
+        for b in range(BLOCKS):
             prods = [held([P, T], F32, f"prod{b}_{r}") for r in range(TOP)]
             res = held([P, T], F32, f"res{b}")
-            if b < N // P - 1:
+            if b < BLOCKS - 1:
                 for r in range(TOP):
                     nc.vector.tensor_tensor(prods[r][:], y[b][:].indirect(pos[r][:]), gates[:, r, :], MULT)
                 by_token = held([P, T], F32, f"by_token{b}")
-                tiles = [slice(j * P, (j + 1) * P) for j in range(T // P)]
-                if b < N // P - 2:
+                one_bank = b < BLOCKS - 2
+                if one_bank:
                     summed = bank_tile(("odd1", "spare0")[b])
-                    sums = [summed[:, cols] for cols in tiles]
+                    sums = [summed[:, cols] for cols in token_tiles]
                     order = [(j, r) for j in range(T // P) for r in range(TOP)]
                 else:
                     sums = [bank_tile(tag)[:, 0:P] for tag in y_tags]
                     order = [(j, r) for r in range(TOP) for j in range(T // P)]
                 for j, r in order:
                     nc.tensor.matmul(
-                        sums[j], lhsT=prods[r][:, tiles[j]], rhs=ident[:], is_transpose=True,
+                        sums[j], lhsT=prods[r][:, token_tiles[j]], rhs=ident[:], is_transpose=True,
                         start=(r == 0), stop=(r == TOP - 1),
                     )
-                if b < N // P - 2:
+                if one_bank:
                     nc.scalar.copy(out=by_token[:], in_=summed[:])
                 else:
-                    for j in range(T // P):
-                        nc.scalar.copy(out=by_token[:, tiles[j]], in_=sums[j])
+                    for j, cols in enumerate(token_tiles):
+                        nc.scalar.copy(out=by_token[:, cols], in_=sums[j])
                 back = bank_tile(("even2", "spare1")[b % 2])
-                for j in range(T // P):
-                    cols = slice(j * P, (j + 1) * P)
+                for cols in token_tiles:
                     nc.tensor.transpose(back[:, cols], by_token[:, cols], ident[:])
                 nc.scalar.copy(out=res[:], in_=back[:])
                 nc.scalar.dma_start(out=out[b * P : (b + 1) * P, :], in_=res[:])
@@ -326,12 +327,10 @@ def tile_moe_hot_mlp_relu_kernel(
                 for r in range(TOP - 1):
                     nc.vector.tensor_tensor(prods[r][:], y[b][:].indirect(pos[r][:]), gates[:, r, :], MULT)
                 nc.vector.tensor_tensor(part[:], prods[0][:], prods[1][:], ADD)
-                half = T // 2
-                for i in range(2):
-                    cols = slice(i * half, (i + 1) * half)
-                    window = y[b][:].indirect(pos[TOP - 1][:, i * half // 16 : (i + 1) * half // 16])
+                halves = [slice(0, T // 2), slice(T // 2, T)]
+                for cols in halves:
+                    window = y[b][:].indirect(pos[TOP - 1][:, cols.start // 16 : cols.stop // 16])
                     nc.vector.tensor_tensor(prods[TOP - 1][:, cols], window, gates[:, TOP - 1, cols], MULT)
-                for i in range(2):
-                    cols = slice(i * half, (i + 1) * half)
+                for cols in halves:
                     nc.vector.tensor_tensor(res[:, cols], part[:, cols], prods[TOP - 1][:, cols], ADD)
                     nc.sync.dma_start(out=out[b * P : (b + 1) * P, cols], in_=res[:, cols])

from contextlib import ExitStack

import concourse.mybir as mybir
from concourse.masks import make_identity

K, T, E, C, H, N, HOT, TOP = 1536, 512, 6, 256, 512, 512, 3, 3
COLD = E - HOT
S = E * C
P = 128
PASSES = K // 512
BLOCKS = N // P
FLOPS = 2 * S * (K * H + H * N)
BYTES = (
    K * T * 33 // 32 + HOT * (K * H + H * N) * 33 // 32 + COLD * (K * H + H * N) * 17 // 32
    + 4 * TOP * T + 2 * P * (S + TOP * T) // 16 + 4 * N * T
)

F32 = mybir.dt.float32
BF16 = mybir.dt.bfloat16
I32 = mybir.dt.int32
U32 = mybir.dt.uint32
U16 = mybir.dt.uint16
U8 = mybir.dt.uint8
FP8X4 = mybir.dt.float8_e4m3fn_x4
FP4X4 = mybir.dt.float4_e2m1fn_x4
RELU = mybir.ActivationFunctionType.Relu
MULT = mybir.AluOpType.mult
ADD = mybir.AluOpType.add

W1H_ROW = 4
W2H_ROW = 8
SHIFT_ROWS = 112
WORD_RING = 2 * PASSES


def tile_moe_hot_mlp_relu_kernel(
    tc, x_words, x_scales, w1h_words, w1h_scales, w2h_words, w2h_scales,
    w1c_words, w1c_scales, w2c_words, w2c_scales, gate, offs, pos1, pos2, pos3, out,
):
    nc = tc.nc
    with ExitStack() as ctx:
        lists = ctx.enter_context(tc.tile_pool(name="lists", bufs=1))
        keep = ctx.enter_context(tc.tile_pool(name="keep", bufs=1))
        big = ctx.enter_context(tc.tile_pool(name="big", bufs=1))
        ring = ctx.enter_context(tc.tile_pool(name="ring", bufs=1))
        psum = ctx.enter_context(tc.psum_pool(name="psum", bufs=1))

        def bank_tile(tag):
            return psum.tile([P, 4 * P], F32, name=tag)

        def held(shape, dtype, name):
            return keep.tile(shape, dtype, name=name, align_bytes=64)

        def zeroed_plane(engine, width, name):
            plane = held([P, width], U8, name)
            engine.memset(plane[:].bitcast(I32), 0)
            return plane

        def load_scale_rows(plane, row, scales):
            rows = scales.bitcast(I32).rearrange("e s b i -> b (e s) i")
            view = plane.bitcast(I32).rearrange("p (a i) -> p a i", i=H // 4)
            for r in range(4):
                nc.sync.dma_start(out=view[row + r : P : 32], in_=rows[r:16:4])

        x_plane = zeroed_plane(nc.gpsimd, T, "x_plane")
        w1h_plane = held([P, HOT * PASSES * H], U8, "w1h_plane")
        half_plane = HOT * PASSES * H // 2
        nc.gpsimd.memset(w1h_plane[:, 0:half_plane].bitcast(I32), 0)
        nc.vector.memset(w1h_plane[:, half_plane:].bitcast(I32), 0)
        w1c_plane = zeroed_plane(nc.vector, COLD * PASSES * H, "w1c_plane")
        cold_planes = {
            (first, s): zeroed_plane(nc.vector, count * C, f"cold_plane{first}_{s}")
            for first, count in ((HOT, 1), (HOT + 1, COLD - 1))
            for s in range(1, PASSES)
        }
        ident = held([P, P], F32, "ident")
        make_identity(nc, ident[:])

        offsets = lists.tile([P, S // 16], U16, name="offsets")
        nc.sync.dma_start(offsets[:], offs)
        x_first = held([P, T], I32, "x_first")
        x_rest = held([P, PASSES - 1, T], I32, "x_rest")
        x_win = [x_first[:]] + [x_rest[:, s, :] for s in range(PASSES - 1)]
        x_source = x_words.rearrange("s p t d -> p s (t d)").bitcast(I32)

        def load_x_scales(queue, q):
            queue.dma_start(
                out=x_plane[:].bitcast(I32)[32 * q : 32 * q + 4 * PASSES, :],
                in_=x_scales.bitcast(I32)[:, 4 * q : 4 * q + 4, :],
            )

        def w1_source(e):
            if e < HOT:
                return w1h_words[e].rearrange("s p i d -> p s (i d)").bitcast(I32)
            return w1c_words[e - HOT].rearrange("s p b -> p s b").bitcast(I32)

        w1 = {}

        def load_w1(e, first, last, tag):
            width = H if e < HOT else H // 2
            w = big.tile([P, last - first, width], I32, name=f"w1_{e}_{first}", tag=tag, align_bytes=64)
            nc.sync.dma_start(out=w[:], in_=w1_source(e)[:, first:last, :])
            for s in range(first, last):
                w1[e, s] = w[:, s - first, :]

        load_x_scales(nc.scalar, 0)
        nc.sync.dma_start(out=x_first[:], in_=x_source[:, 0, :])
        load_x_scales(nc.scalar, 1)
        load_w1(0, 0, 1, "w1_0_first")
        load_x_scales(nc.sync, 2)
        load_x_scales(nc.sync, 3)
        nc.sync.dma_start(out=x_rest[:], in_=x_source[:, 1:PASSES, :])
        load_scale_rows(w1h_plane[:], W1H_ROW, w1h_scales)
        load_w1(0, 1, PASSES, "w1_0_rest")
        load_w1(1, 0, PASSES, "w1_1")
        load_w1(2, 0, PASSES, "w1_2")
        load_scale_rows(w1c_plane[:], 0, w1c_scales)
        load_w1(3, 0, PASSES, "w1_3")
        load_w1(4, 0, PASSES, "w1_4")

        def slots_of(first, count):
            return offsets[:, first // 16 : (first + count) // 16]

        tok_words = {}
        tok_bytes = {}

        def pass_order(e):
            return (1, 2, 0) if e > HOT else (0, 1, 2)

        def gather_words(e, i):
            s = pass_order(e)[i]
            words = ring.tile([P, C], U32, name=f"tok{(e * PASSES + i) % WORD_RING}", align_bytes=64)
            tok_words[e, s] = words
            step = P if (e, i) == (E - 1, PASSES - 1) else C
            for first in range(0, C, step):
                nc.vector.tensor_copy(
                    words[:, first : first + step],
                    x_win[s].bitcast(U32).indirect(slots_of(e * C + first, step)),
                )

        def gather_bytes(e, tile, col):
            tok_bytes[e] = (tile, col)
            nc.vector.tensor_copy(tile[:, col : col + C], x_plane[:].indirect(slots_of(e * C, C)))

        def shift_rows(first, count):
            tile, col = tok_bytes[first]
            for s in range(1, PASSES):
                nc.sync.dma_start(
                    out=cold_planes[first, s][:].bitcast(I32)[0:SHIFT_ROWS, :],
                    in_=tile[:, col : col + count * C].bitcast(I32)[4 * s : 4 * s + SHIFT_ROWS, :],
                )

        def gathers(e):
            if e < HOT:
                tile = ring.tile([P, 2 * C], U8, name=f"tok_bytes{e % 2}", align_bytes=64)
                gather_bytes(e, tile, 0)
            gather_words(e, 0)
            if e == HOT - 1:
                gather_bytes(HOT, tile, C)
                shift_rows(HOT, 1)
            for i in range(1, PASSES):
                gather_words(e, i)
            if e == HOT - 1:
                late = big.tile([P, 2 * C], U8, name="late_bytes", tag="w1_0_rest", align_bytes=64)
                gather_bytes(HOT + 1, late, 0)
                gather_bytes(HOT + 2, late, C)
                shift_rows(HOT + 1, COLD - 1)
                load_w1(E - 1, 0, PASSES, "w1_1")

        def first_layer(e):
            banks = [bank_tile(f"even{e % 3}"), bank_tile(f"odd{e % 2}")]
            if e < E - 1:
                order = [(s, j) for j in range(2) for s in pass_order(e)]
            else:
                order = [(s, j) for s in pass_order(e) for j in range(2)]
            for s, j in order:
                cols = slice(j * P, (j + 1) * P)
                w_cols = slice((e % HOT * PASSES + s) * H, (e % HOT * PASSES + s + 1) * H)
                if e < HOT:
                    tok_scale = tok_bytes[e][0][4 * s : P, cols]
                    w_op = w1[e, s].bitcast(FP8X4)
                    w_scale = w1h_plane[W1H_ROW:P, w_cols]
                else:
                    if s == 0:
                        plane, col = tok_bytes[e]
                    else:
                        plane, col = cold_planes[min(e, HOT + 1), s], max(e - HOT - 1, 0) * C
                    tok_scale = plane[:, col + j * P : col + (j + 1) * P]
                    w_op = w1[e, s].bitcast(FP4X4)
                    w_scale = w1c_plane[:, w_cols]
                nc.tensor.matmul_mx(
                    out=banks[j][:], lhsT=tok_words[e, s][:, cols].bitcast(FP8X4), lhsT_scale=tok_scale,
                    rhs=w_op, rhs_scale=w_scale, start=(s == pass_order(e)[0]), stop=(s == pass_order(e)[-1]),
                )
            hidden = []
            for j in range(2):
                hb = held([P, H], BF16, f"hb{e}_{j}")
                laid = hb[:].rearrange("t (u p d) -> t u p d", u=2, d=2)
                sums = banks[j][:].rearrange("t (p u d) -> t u p d", u=2, d=2)
                if (e, j) == (E - 1, 1):
                    nc.vector.tensor_scalar_max(laid, sums, 0.0)
                else:
                    nc.scalar.activation(out=laid, in_=sums, func=RELU)
                hidden.append(hb)
            return hidden

        def turn_hidden(tiles, name, tag, copy):
            n = len(tiles)
            bank = bank_tile(tag)
            for j, hb in enumerate(tiles):
                pairs = hb[:].bitcast(F32)
                for u in range(2):
                    col = (2 * j + u) * P
                    nc.tensor.transpose(bank[:, col : col + P], pairs[:, u * P : (u + 1) * P], ident[:])
            grouped = held([P, n * H], BF16, name)
            copy(
                out=grouped[:].bitcast(F32).rearrange("p (j t u) -> p j t u", j=n, u=2),
                in_=bank[:, 0 : 2 * n * P].rearrange("p (j u t) -> p j t u", j=n, u=2),
            )
            return grouped

        w2_plane = w1h_plane[:, (HOT - 1) * PASSES * H : HOT * PASSES * H]
        pieces = []
        hidden = []
        for e in range(E):
            gathers(e)
            hidden.append(first_layer(e))
            if e == HOT - 1:
                w2h = ring.tile([P, HOT, N], I32, name="w2h", tag="tok_bytes1", align_bytes=64)
                nc.sync.dma_start(out=w2h[:], in_=w2h_words.rearrange("e s p n d -> p (e s) (n d)").bitcast(I32))
                w2c = big.tile([P, COLD, N // 2], I32, name="w2c", tag="w1_2", align_bytes=64)
                nc.sync.dma_start(out=w2c[:], in_=w2c_words.rearrange("e s p b -> p (e s) b").bitcast(I32))
                load_scale_rows(w2_plane[:], W2H_ROW, w2h_scales)
                load_scale_rows(w2_plane[:], 0, w2c_scales)
            if 0 < e < E - 1:
                grouped = turn_hidden(hidden[e - 1], f"grouped{e - 1}", f"even{e % 3}", nc.scalar.copy)
                pieces.append((e - 1, 0, C, grouped))
        pieces.append((E - 1, 0, P, turn_hidden(hidden[E - 1][0:1], "grouped_a", "spare0", nc.scalar.copy)))
        pieces.append((E - 2, 0, C, turn_hidden(hidden[E - 2], "grouped_4", "even2", nc.vector.tensor_copy)))
        pieces.append((E - 1, P, P, turn_hidden(hidden[E - 1][1:2], "grouped_b", "spare1", nc.scalar.copy)))

        pos = []
        for r, src in enumerate((pos1, pos2, pos3)):
            lst = lists.tile([P, T // 16], U16, name=f"pos{r}")
            nc.sync.dma_start(lst[:], src)
            pos.append(lst)
        gates = big.tile([P, TOP, T], F32, name="gates", tag="w1_3", align_bytes=64)
        nc.sync.dma_start(out=gates[:], in_=gate.rearrange("r p t -> p r t"))

        h_words = [held([P, C], U32, f"h_words{e}") for e in range(E)]
        h_bytes = [held([P, C], U8, f"h_bytes{e}") for e in range(E)]
        for e, first, count, grouped in pieces:
            nc.vector.quantize_mx(
                out=h_words[e][:, first : first + count].bitcast(FP8X4),
                scales=h_bytes[e][:, first : first + count],
                in_=grouped[:],
            )

        def second_layer(bank_cols, e, b, first, count):
            n_cols = slice(e % HOT * N + b * P, e % HOT * N + (b + 1) * P)
            if e < HOT:
                w_op = w2h[:, e, b * P : (b + 1) * P].bitcast(FP8X4)
                w_scale = w2_plane[W2H_ROW:P, n_cols]
            else:
                w_op = w2c[:, e - HOT, b * P // 2 : (b + 1) * P // 2].bitcast(FP4X4)
                w_scale = w2_plane[:, n_cols]
            nc.tensor.matmul_mx(
                out=bank_cols, lhsT=w_op, lhsT_scale=w_scale,
                rhs=h_words[e][:, first : first + count].bitcast(FP8X4),
                rhs_scale=h_bytes[e][:, first : first + count], start=True, stop=True,
            )

        y = [held([P, S], F32, f"y{b}") for b in range(BLOCKS)]
        y_tags = ["spare2", "even0", "even1", "odd0"]
        turn = 0
        for b in range(BLOCKS):
            for pair in range(E // 2):
                bank = bank_tile(y_tags[turn % len(y_tags)])
                turn = turn + 1
                base = pair * 2 * C
                if b == 0 and pair == E // 2 - 1:
                    second_layer(bank[:, 0:C], E - 2, b, 0, C)
                    second_layer(bank[:, C : C + P], E - 1, b, 0, P)
                    nc.scalar.copy(out=y[b][:, base : base + C + P], in_=bank[:, 0 : C + P])
                    last = bank_tile(y_tags[turn % len(y_tags)])
                    turn = turn + 1
                    second_layer(last[:, 0:P], E - 1, b, P, P)
                    nc.vector.tensor_copy(out=y[b][:, S - P : S], in_=last[:, 0:P])
                else:
                    for i in range(2):
                        second_layer(bank[:, i * C : (i + 1) * C], 2 * pair + i, b, 0, C)
                    nc.scalar.copy(out=y[b][:, base : base + 2 * C], in_=bank[:])

        token_tiles = [slice(j * P, (j + 1) * P) for j in range(T // P)]
        for b in range(BLOCKS):
            prods = [held([P, T], F32, f"prod{b}_{r}") for r in range(TOP)]
            res = held([P, T], F32, f"res{b}")
            if b < BLOCKS - 1:
                for r in range(TOP):
                    nc.vector.tensor_tensor(prods[r][:], y[b][:].indirect(pos[r][:]), gates[:, r, :], MULT)
                by_token = held([P, T], F32, f"by_token{b}")
                one_bank = b < BLOCKS - 2
                if one_bank:
                    summed = bank_tile(("odd1", "spare0")[b])
                    sums = [summed[:, cols] for cols in token_tiles]
                    order = [(j, r) for j in range(T // P) for r in range(TOP)]
                else:
                    sums = [bank_tile(tag)[:, 0:P] for tag in y_tags]
                    order = [(j, r) for r in range(TOP) for j in range(T // P)]
                for j, r in order:
                    nc.tensor.matmul(
                        sums[j], lhsT=prods[r][:, token_tiles[j]], rhs=ident[:], is_transpose=True,
                        start=(r == 0), stop=(r == TOP - 1),
                    )
                if one_bank:
                    nc.scalar.copy(out=by_token[:], in_=summed[:])
                else:
                    for j, cols in enumerate(token_tiles):
                        nc.scalar.copy(out=by_token[:, cols], in_=sums[j])
                back = bank_tile(("even2", "spare1")[b % 2])
                for cols in token_tiles:
                    nc.tensor.transpose(back[:, cols], by_token[:, cols], ident[:])
                nc.scalar.copy(out=res[:], in_=back[:])
                nc.scalar.dma_start(out=out[b * P : (b + 1) * P, :], in_=res[:])
            else:
                part = held([P, T], F32, "part")
                for r in range(TOP - 1):
                    nc.vector.tensor_tensor(prods[r][:], y[b][:].indirect(pos[r][:]), gates[:, r, :], MULT)
                nc.vector.tensor_tensor(part[:], prods[0][:], prods[1][:], ADD)
                halves = [slice(0, T // 2), slice(T // 2, T)]
                for cols in halves:
                    window = y[b][:].indirect(pos[TOP - 1][:, cols.start // 16 : cols.stop // 16])
                    nc.vector.tensor_tensor(prods[TOP - 1][:, cols], window, gates[:, TOP - 1, cols], MULT)
                for cols in halves:
                    nc.vector.tensor_tensor(res[:, cols], part[:, cols], prods[TOP - 1][:, cols], ADD)
                    nc.sync.dma_start(out=out[b * P : (b + 1) * P, cols], in_=res[:, cols])
